import numpy as np
import ml_dtypes


def mxq(x, axis, fmt="e4m3"):
    dtype, down = {"e4m3": (ml_dtypes.float8_e4m3fn, 7), "e5m2": (ml_dtypes.float8_e5m2, 14)}[fmt]
    v = np.moveaxis(np.asarray(x, np.float32).astype(ml_dtypes.bfloat16).astype(np.float64), axis, -1)
    blocks = v.reshape(v.shape[:-1] + (-1, 32))
    amax = np.abs(blocks).max(-1, keepdims=True)
    byte = np.maximum(np.where(amax > 0, np.frexp(amax)[1] - 1 + 127, 0) - down, 1)
    scale = np.exp2(byte - 127.0)
    codes = (blocks / scale).astype(np.float32).astype(dtype).astype(np.float64)
    return np.moveaxis((codes * scale).reshape(v.shape), -1, axis)


WIDE = False


def mx_kscale(k):
    if not WIDE:
        return np.ones(k)
    levels = np.array([10, -10, 5, -5, 0])
    if k % 512:
        return np.exp2(np.random.permutation(np.resize(levels, k // 32))).repeat(32)
    a = np.empty((k // 512, 16))
    for p in range(k // 512):
        a[p, :8] = np.random.permutation(np.resize(levels, 8))
        for g in range(8):
            far = levels[np.abs(levels - a[p, g]) >= 10]
            a[p, g + 8] = far[np.random.randint(len(far))]
    return np.exp2(a.ravel()).repeat(32)


def f64(x):
    return np.asarray(x).astype(np.float64)


def striped(idx):
    return np.tile(idx.reshape(-1, 16).T, (8, 1)).astype(np.uint16)


def unstriped(offs):
    return offs[:16].T.reshape(-1).astype(np.int64)


def relu(v):
    return np.maximum(v, 0.0)


K, T, E, C, N = 1024, 1024, 8, 128, 256


def by_expert(wq, xq):
    return np.concatenate([wq[e].T @ xq[:, e * C:(e + 1) * C] for e in range(E)], axis=1)


def setup_inputs():
    n = np.random.standard_normal
    s = mx_kscale(K)[:, None]
    return {
        "xT": (n((K, T)) * s).astype(np.float32),
        "w": (n((E, K, N)) / np.sqrt(K) / s[None]).astype(np.float32),
        "b": (0.3 * n((N, E))).astype(np.float32),
        "gate": np.tile(np.random.uniform(0.2, 1.0, E * C), (N, 1)).astype(np.float32),
        "offs": striped(np.random.permutation(T)[:E * C]),
    }


def reference(xT, w, b, gate, offs):
    idx = unstriped(offs)
    xq = mxq(f64(xT)[:, idx], 0, "e4m3")
    y = by_expert(mxq(f64(w), 1, "e4m3"), xq)
    y = relu(y + np.repeat(f64(b), C, axis=1))
    out = np.zeros((N, T))
    out[:, idx] = f64(gate) * y
    return out

@@ -1,0 +1,140 @@
+from contextlib import ExitStack
+
+import concourse.mybir as mybir
+
+K, T, E, C, N = 1024, 1024, 8, 128, 256
+FLOPS = 2 * E * C * K * N
+
+F32 = mybir.dt.float32
+BF16 = mybir.dt.bfloat16
+U32 = mybir.dt.uint32
+U16 = mybir.dt.uint16
+U8 = mybir.dt.uint8
+FP8X4 = mybir.dt.float8_e4m3fn_x4
+MULT = mybir.AluOpType.mult
+RELU = mybir.ActivationFunctionType.Relu
+
+P = 128
+PACK = 4
+K_PASS = P * PACK
+PASSES = K // K_PASS
+HALVES = N // P
+GATHER = 512
+N_GATHER = E * C // GATHER
+SCATTER = 256
+EXPERTS_A_SCATTER = SCATTER // C
+
+
+def interleave(engine_copy, dst, src):
+    engine_copy(
+        out=dst.rearrange("p (c i) t -> p c t i", i=4),
+        in_=src.rearrange("p t (c i) -> p c t i", i=4),
+    )
+
+
+def tile_routed_moe_kernel(tc, xT, w, b, gate, offs, out):
+    nc = tc.nc
+    with ExitStack() as ctx:
+        keep = ctx.enter_context(tc.tile_pool(name="keep", bufs=1))
+        ring = ctx.enter_context(tc.tile_pool(name="ring", bufs=4))
+        psum = ctx.enter_context(tc.psum_pool(name="psum", bufs=4))
+
+        offsets = keep.tile([P, E * C // 16], U16, name="offsets")
+        nc.sync.dma_start(offsets[:], offs)
+
+        x_view = xT.rearrange("(g p t) n -> g p t n", p=P, t=PACK)
+        planes = [[keep.tile([P, T], F32, name="plane%d%d" % (g, t)) for t in range(PACK)] for g in range(PASSES)]
+        for g in range(PASSES):
+            for t in range(PACK):
+                nc.sync.dma_start(planes[g][t][:], x_view[g, :, t, :])
+
+        bias = keep.tile([P, HALVES, E], F32, name="bias")
+        nc.sync.dma_start(bias[:], b.rearrange("(h p) e -> p h e", p=P))
+
+        w_raw = [[keep.tile([P, PACK, N], F32, name="wraw%d%d" % (e, g)) for g in range(PASSES)] for e in range(E)]
+        gates = [keep.tile([P, E * C], F32, name="gate%d" % h) for h in range(HALVES)]
+
+        def load_w(e):
+            for g in range(PASSES):
+                nc.sync.dma_start(
+                    w_raw[e][g][:],
+                    w[e, g * K_PASS : (g + 1) * K_PASS, :].rearrange("(p j) n -> p j n", j=PACK),
+                )
+
+        load_w(0)
+        load_w(1)
+        for h in range(HALVES):
+            nc.sync.dma_start(gates[h][:], gate[h * P : (h + 1) * P, :])
+        for e in range(2, E):
+            load_w(e)
+
+        warm = keep.tile([P, 1], F32, name="warm")
+        nc.vector.memset(warm[:], 0.0)
+        warm_out = keep.tile([P, 1], F32, name="warm_out")
+        nc.scalar.activation(out=warm_out[:], in_=warm[:], func=RELU)
+
+        x_codes = keep.tile([P, PASSES, E * C], U32, name="x_codes", align_bytes=64)
+        x_scales = keep.tile([P, PASSES, E * C], U8, name="x_scales", align_bytes=64)
+        w_codes = [keep.tile([P, PASSES, N], U32, name="w_codes%d" % e, align_bytes=64) for e in range(E)]
+        w_scales = [keep.tile([P, PASSES, N], U8, name="w_scales%d" % e, align_bytes=64) for e in range(E)]
+        windows = [keep.tile([P, T], F32, name="window%d" % h) for h in range(HALVES)]
+
+        for g in range(PASSES):
+            gathered = [ring.tile([P, PACK, GATHER], F32, name="gathered") for s in range(N_GATHER)]
+            for t in range(PACK):
+                for s in range(N_GATHER):
+                    nc.vector.tensor_copy(
+                        gathered[s][:, t, :],
+                        planes[g][t][:].indirect(offsets[:, s * GATHER // 16 : (s + 1) * GATHER // 16]),
+                    )
+            for s in range(N_GATHER):
+                x_bf = ring.tile([P, GATHER, PACK], BF16, name="x_bf", align_bytes=64)
+                interleave(nc.scalar.copy, x_bf[:], gathered[s][:])
+                cols = slice(s * GATHER, (s + 1) * GATHER)
+                nc.vector.quantize_mx(
+                    out=x_codes[:, g, cols].bitcast(FP8X4),
+                    scales=x_scales[:, g, cols],
+                    in_=x_bf[:].rearrange("p c t -> p (c t)"),
+                )
+
+        for pair in range(E // EXPERTS_A_SCATTER):
+            experts = range(pair * EXPERTS_A_SCATTER, (pair + 1) * EXPERTS_A_SCATTER)
+            for e in experts:
+                for g in range(PASSES):
+                    w_bf = ring.tile([P, N, PACK], BF16, name="w_bf", align_bytes=64)
+                    interleave(nc.scalar.copy, w_bf[:], w_raw[e][g][:])
+                    nc.vector.quantize_mx(
+                        out=w_codes[e][:, g, :].bitcast(FP8X4),
+                        scales=w_scales[e][:, g, :],
+                        in_=w_bf[:].rearrange("p c t -> p (c t)"),
+                    )
+            for h in range(HALVES):
+                acc = psum.tile([P, SCATTER], F32, name="acc")
+                y = ring.tile([P, SCATTER], F32, name="y")
+                for i, e in enumerate(experts):
+                    for g in range(PASSES):
+                        nc.tensor.matmul_mx(
+                            out=acc[:, i * C : (i + 1) * C],
+                            lhsT=w_codes[e][:, g, h * P : (h + 1) * P].bitcast(FP8X4),
+                            lhsT_scale=w_scales[e][:, g, h * P : (h + 1) * P],
+                            rhs=x_codes[:, g, e * C : (e + 1) * C].bitcast(FP8X4),
+                            rhs_scale=x_scales[:, g, e * C : (e + 1) * C],
+                            start=(g == 0),
+                            stop=(g == PASSES - 1),
+                        )
+                for i, e in enumerate(experts):
+                    nc.scalar.activation(
+                        out=y[:, i * C : (i + 1) * C],
+                        in_=acc[:, i * C : (i + 1) * C],
+                        func=RELU,
+                        bias=bias[:, h, e : e + 1],
+                    )
+                nc.vector.tensor_tensor(
+                    windows[h][:].indirect(offsets[:, pair * SCATTER // 16 : (pair + 1) * SCATTER // 16]),
+                    y[:],
+                    gates[h][:, pair * SCATTER : (pair + 1) * SCATTER],
+                    MULT,
+                )
+
+        for h in range(HALVES):
+            nc.sync.dma_start(out[h * P : (h + 1) * P, :], windows[h][:])

@@ -12,7 +12,9 @@ U16 = mybir.dt.uint16
 U8 = mybir.dt.uint8
 FP8X4 = mybir.dt.float8_e4m3fn_x4
 MULT = mybir.AluOpType.mult
+ADD = mybir.AluOpType.add
 RELU = mybir.ActivationFunctionType.Relu
+COPY = mybir.ActivationFunctionType.Copy
 
 P = 128
 PACK = 4
@@ -21,52 +23,44 @@ PASSES = K // K_PASS
 HALVES = N // P
 GATHER = 512
 N_GATHER = E * C // GATHER
-SCATTER = 256
-EXPERTS_A_SCATTER = SCATTER // C
-
-
-def interleave(engine_copy, dst, src):
-    engine_copy(
-        out=dst.rearrange("p (c i) t -> p c t i", i=4),
-        in_=src.rearrange("p t (c i) -> p c t i", i=4),
-    )
+LEAD = 2
+VECTOR_EXPERTS = (0, 1)
+GATES_AFTER = 3
+W_BYTES = PASSES * PACK * N * 4
+Y_BYTES = C * 4
 
 
 def tile_routed_moe_kernel(tc, xT, w, b, gate, offs, out):
     nc = tc.nc
     with ExitStack() as ctx:
         keep = ctx.enter_context(tc.tile_pool(name="keep", bufs=1))
-        ring = ctx.enter_context(tc.tile_pool(name="ring", bufs=4))
-        psum = ctx.enter_context(tc.psum_pool(name="psum", bufs=4))
+        shared = ctx.enter_context(tc.tile_pool(name="shared", bufs=1))
+        ring = ctx.enter_context(tc.tile_pool(name="ring", bufs=6))
+        psum = ctx.enter_context(tc.psum_pool(name="psum", bufs=8))
 
         offsets = keep.tile([P, E * C // 16], U16, name="offsets")
         nc.sync.dma_start(offsets[:], offs)
 
         x_view = xT.rearrange("(g p t) n -> g p t n", p=P, t=PACK)
         planes = [[keep.tile([P, T], F32, name="plane%d%d" % (g, t)) for t in range(PACK)] for g in range(PASSES)]
-        for g in range(PASSES):
-            for t in range(PACK):
+        for t in range(PACK):
+            for g in range(PASSES):
                 nc.sync.dma_start(planes[g][t][:], x_view[g, :, t, :])
 
         bias = keep.tile([P, HALVES, E], F32, name="bias")
         nc.sync.dma_start(bias[:], b.rearrange("(h p) e -> p h e", p=P))
-
-        w_raw = [[keep.tile([P, PACK, N], F32, name="wraw%d%d" % (e, g)) for g in range(PASSES)] for e in range(E)]
         gates = [keep.tile([P, E * C], F32, name="gate%d" % h) for h in range(HALVES)]
 
-        def load_w(e):
+        w_raw = [shared.tile([P, PASSES, PACK, N], F32, name="wraw%d" % e, offset=e * W_BYTES) for e in range(E)]
+        for e in range(E):
+            if e == GATES_AFTER:
+                for h in range(HALVES):
+                    nc.sync.dma_start(gates[h][:], gate[h * P : (h + 1) * P, :])
             for g in range(PASSES):
                 nc.sync.dma_start(
-                    w_raw[e][g][:],
+                    w_raw[e][:, g, :, :],
                     w[e, g * K_PASS : (g + 1) * K_PASS, :].rearrange("(p j) n -> p j n", j=PACK),
                 )
-
-        load_w(0)
-        load_w(1)
-        for h in range(HALVES):
-            nc.sync.dma_start(gates[h][:], gate[h * P : (h + 1) * P, :])
-        for e in range(2, E):
-            load_w(e)
 
         warm = keep.tile([P, 1], F32, name="warm")
         nc.vector.memset(warm[:], 0.0)
@@ -78,63 +72,86 @@ def tile_routed_moe_kernel(tc, xT, w, b, gate, offs, out):
         w_codes = [keep.tile([P, PASSES, N], U32, name="w_codes%d" % e, align_bytes=64) for e in range(E)]
         w_scales = [keep.tile([P, PASSES, N], U8, name="w_scales%d" % e, align_bytes=64) for e in range(E)]
         windows = [keep.tile([P, T], F32, name="window%d" % h) for h in range(HALVES)]
+        x_bf = [
+            [keep.tile([P, GATHER, PACK], BF16, name="x_bf%d%d" % (g, s), align_bytes=64) for s in range(N_GATHER)]
+            for g in range(PASSES)
+        ]
+        x16 = keep.tile([P, PACK, T], BF16, name="x16")
+        picked = [keep.tile([P, PACK, GATHER], F32, name="picked%d" % s) for s in range(N_GATHER)]
 
-        for g in range(PASSES):
-            gathered = [ring.tile([P, PACK, GATHER], F32, name="gathered") for s in range(N_GATHER)]
-            for t in range(PACK):
-                for s in range(N_GATHER):
-                    nc.vector.tensor_copy(
-                        gathered[s][:, t, :],
-                        planes[g][t][:].indirect(offsets[:, s * GATHER // 16 : (s + 1) * GATHER // 16]),
-                    )
-            for s in range(N_GATHER):
-                x_bf = ring.tile([P, GATHER, PACK], BF16, name="x_bf", align_bytes=64)
-                interleave(nc.scalar.copy, x_bf[:], gathered[s][:])
-                cols = slice(s * GATHER, (s + 1) * GATHER)
-                nc.vector.quantize_mx(
-                    out=x_codes[:, g, cols].bitcast(FP8X4),
-                    scales=x_scales[:, g, cols],
-                    in_=x_bf[:].rearrange("p c t -> p (c t)"),
+        def list_slice(s):
+            return offsets[:, s * GATHER // 16 : (s + 1) * GATHER // 16]
+
+        def quantise_x(g, s):
+            cols = slice(s * GATHER, (s + 1) * GATHER)
+            nc.vector.quantize_mx(
+                out=x_codes[:, g, cols].bitcast(FP8X4),
+                scales=x_scales[:, g, cols],
+                in_=x_bf[g][s][:].rearrange("p c t -> p (c t)"),
+            )
+
+        def expert_weights(e):
+            w_bf = ring.tile([P, PASSES, N, PACK], BF16, name="w_bf", align_bytes=64)
+            copy = nc.vector.tensor_copy if e in VECTOR_EXPERTS else nc.scalar.copy
+            for g in range(PASSES):
+                copy(
+                    out=w_bf[:, g, :, :].rearrange("p (c i) t -> p c t i", i=4),
+                    in_=w_raw[e][:, g, :, :].rearrange("p t (c i) -> p c t i", i=4),
                 )
+            return w_bf
 
-        for pair in range(E // EXPERTS_A_SCATTER):
-            experts = range(pair * EXPERTS_A_SCATTER, (pair + 1) * EXPERTS_A_SCATTER)
-            for e in experts:
-                for g in range(PASSES):
-                    w_bf = ring.tile([P, N, PACK], BF16, name="w_bf", align_bytes=64)
-                    interleave(nc.scalar.copy, w_bf[:], w_raw[e][g][:])
-                    nc.vector.quantize_mx(
-                        out=w_codes[e][:, g, :].bitcast(FP8X4),
-                        scales=w_scales[e][:, g, :],
-                        in_=w_bf[:].rearrange("p c t -> p (c t)"),
-                    )
+        def quantise_w(e, w_bf):
+            nc.vector.quantize_mx(
+                out=w_codes[e][:].rearrange("p g n -> p (g n)").bitcast(FP8X4),
+                scales=w_scales[e][:].rearrange("p g n -> p (g n)"),
+                in_=w_bf[:].rearrange("p g c t -> p (g c t)"),
+            )
+
+        for t in range(PACK):
+            for s in range(N_GATHER):
+                nc.vector.tensor_copy(picked[s][:, t, :], planes[0][t][:].indirect(list_slice(s)))
+            nc.gpsimd.tensor_scalar(out=x16[:, t, :], in0=planes[1][t][:], scalar1=1.0, scalar2=0.0, op0=MULT, op1=ADD)
+            for s in range(N_GATHER):
+                nc.scalar.activation(out=x_bf[1][s][:, :, t], in_=x16[:, t, :].indirect(list_slice(s)), func=COPY)
+        for s in range(N_GATHER):
+            nc.vector.tensor_copy(
+                out=x_bf[0][s][:].rearrange("p (c i) t -> p c t i", i=4),
+                in_=picked[s][:].rearrange("p t (c i) -> p c t i", i=4),
+            )
+        first_w = [expert_weights(e) for e in range(LEAD)]
+        for s in range(N_GATHER):
+            quantise_x(0, s)
+        for e in range(LEAD):
+            quantise_w(e, first_w[e])
+        for s in range(N_GATHER):
+            quantise_x(1, s)
+
+        for e in range(E):
+            if e + LEAD < E:
+                quantise_w(e + LEAD, expert_weights(e + LEAD))
+            ys = []
             for h in range(HALVES):
-                acc = psum.tile([P, SCATTER], F32, name="acc")
-                y = ring.tile([P, SCATTER], F32, name="y")
-                for i, e in enumerate(experts):
-                    for g in range(PASSES):
-                        nc.tensor.matmul_mx(
-                            out=acc[:, i * C : (i + 1) * C],
-                            lhsT=w_codes[e][:, g, h * P : (h + 1) * P].bitcast(FP8X4),
-                            lhsT_scale=w_scales[e][:, g, h * P : (h + 1) * P],
-                            rhs=x_codes[:, g, e * C : (e + 1) * C].bitcast(FP8X4),
-                            rhs_scale=x_scales[:, g, e * C : (e + 1) * C],
-                            start=(g == 0),
-                            stop=(g == PASSES - 1),
-                        )
-                for i, e in enumerate(experts):
-                    nc.scalar.activation(
-                        out=y[:, i * C : (i + 1) * C],
-                        in_=acc[:, i * C : (i + 1) * C],
-                        func=RELU,
-                        bias=bias[:, h, e : e + 1],
+                acc = psum.tile([P, C], F32, name="acc")
+                for g in range(PASSES):
+                    nc.tensor.matmul_mx(
+                        out=acc[:],
+                        lhsT=w_codes[e][:, g, h * P : (h + 1) * P].bitcast(FP8X4),
+                        lhsT_scale=w_scales[e][:, g, h * P : (h + 1) * P],
+                        rhs=x_codes[:, g, e * C : (e + 1) * C].bitcast(FP8X4),
+                        rhs_scale=x_scales[:, g, e * C : (e + 1) * C],
+                        start=(g == 0),
+                        stop=(g == PASSES - 1),
                     )
+                place = min(e + LEAD + 1, E + 1) * W_BYTES - (HALVES - h) * Y_BYTES if e + LEAD < E else E * W_BYTES + ((e + LEAD - E) * HALVES + h) * Y_BYTES
+                y = shared.tile([P, C], F32, name="y%d%d" % (e, h), offset=place)
+                nc.scalar.activation(out=y[:], in_=acc[:], func=RELU, bias=bias[:, h, e : e + 1])
+                ys.append(y)
+            for h in range(HALVES):
                 nc.vector.tensor_tensor(
-                    windows[h][:].indirect(offsets[:, pair * SCATTER // 16 : (pair + 1) * SCATTER // 16]),
-                    y[:],
-                    gates[h][:, pair * SCATTER : (pair + 1) * SCATTER],
+                    windows[h][:].indirect(offsets[:, e * C // 16 : (e + 1) * C // 16]),
+                    ys[h][:],
+                    gates[h][:, e * C : (e + 1) * C],
                     MULT,
                 )
-
         for h in range(HALVES):
             nc.sync.dma_start(out[h * P : (h + 1) * P, :], windows[h][:])

@@ -77,7 +77,16 @@ def tile_routed_moe_kernel(tc, xT, w, b, gate, offs, out):
             for g in range(PASSES)
         ]
         x16 = keep.tile([P, PACK, T], BF16, name="x16")
-        picked = [keep.tile([P, PACK, GATHER], F32, name="picked%d" % s) for s in range(N_GATHER)]
+        pairs = [
+            [keep.tile([P, PACK // 2, GATHER, 2], BF16, name="pairs%d%d" % (g, s), align_bytes=64) for s in range(N_GATHER)]
+            for g in range(PASSES)
+        ]
+
+        def weave(copy, g, s):
+            copy(
+                out=x_bf[g][s][:].rearrange("p c t -> p (c t)").bitcast(F32).rearrange("p (c u) -> p c u", u=2),
+                in_=pairs[g][s][:].rearrange("p u c i -> p (u c i)").bitcast(F32).rearrange("p (u c) -> p c u", u=2),
+            )
 
         def list_slice(s):
             return offsets[:, s * GATHER // 16 : (s + 1) * GATHER // 16]
@@ -109,15 +118,14 @@ def tile_routed_moe_kernel(tc, xT, w, b, gate, offs, out):
 
         for t in range(PACK):
             for s in range(N_GATHER):
-                nc.vector.tensor_copy(picked[s][:, t, :], planes[0][t][:].indirect(list_slice(s)))
+                nc.vector.tensor_copy(pairs[0][s][:, t // 2, :, t % 2], planes[0][t][:].indirect(list_slice(s)))
             nc.gpsimd.tensor_scalar(out=x16[:, t, :], in0=planes[1][t][:], scalar1=1.0, scalar2=0.0, op0=MULT, op1=ADD)
             for s in range(N_GATHER):
-                nc.scalar.activation(out=x_bf[1][s][:, :, t], in_=x16[:, t, :].indirect(list_slice(s)), func=COPY)
+                nc.scalar.activation(out=pairs[1][s][:, t // 2, :, t % 2], in_=x16[:, t, :].indirect(list_slice(s)), func=COPY)
         for s in range(N_GATHER):
-            nc.vector.tensor_copy(
-                out=x_bf[0][s][:].rearrange("p (c i) t -> p c t i", i=4),
-                in_=picked[s][:].rearrange("p t (c i) -> p c t i", i=4),
-            )
+            weave(nc.scalar.copy, 1, s)
+        for s in range(N_GATHER):
+            weave(nc.vector.tensor_copy, 0, s)
         first_w = [expert_weights(e) for e in range(LEAD)]
         for s in range(N_GATHER):
             quantise_x(0, s)

@@ -24,7 +24,7 @@ HALVES = N // P
 GATHER = 512
 N_GATHER = E * C // GATHER
 LEAD = 2
-VECTOR_EXPERTS = (0, 1)
+VECTOR_BLOCKS = ((0, 0), (0, 1), (1, 0), (1, 1), (4, 0), (7, 0))
 GATES_AFTER = 3
 W_BYTES = PASSES * PACK * N * 4
 Y_BYTES = C * 4
@@ -101,8 +101,8 @@ def tile_routed_moe_kernel(tc, xT, w, b, gate, offs, out):
 
         def expert_weights(e):
             w_bf = ring.tile([P, PASSES, N, PACK], BF16, name="w_bf", align_bytes=64)
-            copy = nc.vector.tensor_copy if e in VECTOR_EXPERTS else nc.scalar.copy
             for g in range(PASSES):
+                copy = nc.vector.tensor_copy if (e, g) in VECTOR_BLOCKS else nc.scalar.copy
                 copy(
                     out=w_bf[:, g, :, :].rearrange("p (c i) t -> p c t i", i=4),
                     in_=w_raw[e][:, g, :, :].rearrange("p t (c i) -> p c t i", i=4),

@@ -24,8 +24,11 @@ HALVES = N // P
 GATHER = 512
 N_GATHER = E * C // GATHER
 LEAD = 2
-VECTOR_BLOCKS = ((0, 0), (0, 1), (1, 0), (1, 1), (4, 0), (7, 0))
+VECTOR_BLOCKS = ((0, 0), (0, 1), (1, 0), (1, 1), (4, 0))
+WINDOW = T * 11 // 8
 GATES_AFTER = 3
+GATE_PARTS = 2
+GATE_EXPERTS = E // GATE_PARTS
 W_BYTES = PASSES * PACK * N * 4
 Y_BYTES = C * 4
 
@@ -42,25 +45,34 @@ def tile_routed_moe_kernel(tc, xT, w, b, gate, offs, out):
         nc.sync.dma_start(offsets[:], offs)
 
         x_view = xT.rearrange("(g p t) n -> g p t n", p=P, t=PACK)
-        planes = [[keep.tile([P, T], F32, name="plane%d%d" % (g, t)) for t in range(PACK)] for g in range(PASSES)]
+        planes = [[keep.tile([P, T if g else WINDOW], F32, name="plane%d%d" % (g, t)) for t in range(PACK)] for g in range(PASSES)]
+        for t in range(PACK):
+            nc.gpsimd.memset(planes[0][t][:, T:], 0.0)
         for t in range(PACK):
             for g in range(PASSES):
-                nc.sync.dma_start(planes[g][t][:], x_view[g, :, t, :])
+                nc.sync.dma_start(planes[g][t][:, :T], x_view[g, :, t, :])
 
         bias = keep.tile([P, HALVES, E], F32, name="bias")
         nc.sync.dma_start(bias[:], b.rearrange("(h p) e -> p h e", p=P))
-        gates = [keep.tile([P, E * C], F32, name="gate%d" % h) for h in range(HALVES)]
+        gates = [keep.tile([P, HALVES, GATE_EXPERTS * C], F32, name="gates%d" % part) for part in range(GATE_PARTS)]
+        gate_view = gate.rearrange("(h p) s -> p h s", p=P)
+
+        def load_gate(part):
+            nc.sync.dma_start(gates[part][:], gate_view[:, :, part * GATE_EXPERTS * C : (part + 1) * GATE_EXPERTS * C])
 
         w_raw = [shared.tile([P, PASSES, PACK, N], F32, name="wraw%d" % e, offset=e * W_BYTES) for e in range(E)]
         for e in range(E):
             if e == GATES_AFTER:
-                for h in range(HALVES):
-                    nc.sync.dma_start(gates[h][:], gate[h * P : (h + 1) * P, :])
-            for g in range(PASSES):
-                nc.sync.dma_start(
-                    w_raw[e][:, g, :, :],
-                    w[e, g * K_PASS : (g + 1) * K_PASS, :].rearrange("(p j) n -> p j n", j=PACK),
-                )
+                load_gate(0)
+            if e < E - 1:
+                nc.sync.dma_start(w_raw[e][:], w[e].rearrange("(g p j) n -> p g j n", p=P, j=PACK))
+            else:
+                for g in range(PASSES):
+                    nc.sync.dma_start(
+                        w_raw[e][:, g, :, :],
+                        w[e, g * K_PASS : (g + 1) * K_PASS, :].rearrange("(p j) n -> p j n", j=PACK),
+                    )
+        load_gate(1)
 
         warm = keep.tile([P, 1], F32, name="warm")
         nc.vector.memset(warm[:], 0.0)
@@ -72,13 +84,14 @@ def tile_routed_moe_kernel(tc, xT, w, b, gate, offs, out):
         w_codes = [keep.tile([P, PASSES, N], U32, name="w_codes%d" % e, align_bytes=64) for e in range(E)]
         w_scales = [keep.tile([P, PASSES, N], U8, name="w_scales%d" % e, align_bytes=64) for e in range(E)]
         windows = [keep.tile([P, T], F32, name="window%d" % h) for h in range(HALVES)]
+        units = [[(0, E * C)], [(s * GATHER, GATHER) for s in range(N_GATHER)]]
         x_bf = [
-            [keep.tile([P, GATHER, PACK], BF16, name="x_bf%d%d" % (g, s), align_bytes=64) for s in range(N_GATHER)]
+            [keep.tile([P, n, PACK], BF16, name="x_bf%d%d" % (g, first), align_bytes=64) for first, n in units[g]]
             for g in range(PASSES)
         ]
         x16 = keep.tile([P, PACK, T], BF16, name="x16")
         pairs = [
-            [keep.tile([P, PACK // 2, GATHER, 2], BF16, name="pairs%d%d" % (g, s), align_bytes=64) for s in range(N_GATHER)]
+            [keep.tile([P, PACK // 2, n, 2], BF16, name="pairs%d%d" % (g, first), align_bytes=64) for first, n in units[g]]
             for g in range(PASSES)
         ]
 
@@ -88,11 +101,13 @@ def tile_routed_moe_kernel(tc, xT, w, b, gate, offs, out):
                 in_=pairs[g][s][:].rearrange("p u c i -> p (u c i)").bitcast(F32).rearrange("p (u c) -> p c u", u=2),
             )
 
-        def list_slice(s):
-            return offsets[:, s * GATHER // 16 : (s + 1) * GATHER // 16]
+        def list_slice(g, s):
+            first, n = units[g][s]
+            return offsets[:, first // 16 : (first + n) // 16]
 
         def quantise_x(g, s):
-            cols = slice(s * GATHER, (s + 1) * GATHER)
+            first, n = units[g][s]
+            cols = slice(first, first + n)
             nc.vector.quantize_mx(
                 out=x_codes[:, g, cols].bitcast(FP8X4),
                 scales=x_scales[:, g, cols],
@@ -101,6 +116,12 @@ def tile_routed_moe_kernel(tc, xT, w, b, gate, offs, out):
 
         def expert_weights(e):
             w_bf = ring.tile([P, PASSES, N, PACK], BF16, name="w_bf", align_bytes=64)
+            if all((e, g) in VECTOR_BLOCKS for g in range(PASSES)):
+                nc.vector.tensor_copy(
+                    out=w_bf[:].rearrange("p g (c i) t -> p g c t i", i=4),
+                    in_=w_raw[e][:].rearrange("p g t (c i) -> p g c t i", i=4),
+                )
+                return w_bf
             for g in range(PASSES):
                 copy = nc.vector.tensor_copy if (e, g) in VECTOR_BLOCKS else nc.scalar.copy
                 copy(
@@ -117,18 +138,15 @@ def tile_routed_moe_kernel(tc, xT, w, b, gate, offs, out):
             )
 
         for t in range(PACK):
-            for s in range(N_GATHER):
-                nc.vector.tensor_copy(pairs[0][s][:, t // 2, :, t % 2], planes[0][t][:].indirect(list_slice(s)))
+            nc.vector.tensor_copy(pairs[0][0][:, t // 2, :, t % 2], planes[0][t][:].indirect(list_slice(0, 0)))
             nc.gpsimd.tensor_scalar(out=x16[:, t, :], in0=planes[1][t][:], scalar1=1.0, scalar2=0.0, op0=MULT, op1=ADD)
             for s in range(N_GATHER):
-                nc.scalar.activation(out=pairs[1][s][:, t // 2, :, t % 2], in_=x16[:, t, :].indirect(list_slice(s)), func=COPY)
+                nc.scalar.activation(out=pairs[1][s][:, t // 2, :, t % 2], in_=x16[:, t, :].indirect(list_slice(1, s)), func=COPY)
         for s in range(N_GATHER):
             weave(nc.scalar.copy, 1, s)
-        for s in range(N_GATHER):
-            weave(nc.vector.tensor_copy, 0, s)
+        weave(nc.vector.tensor_copy, 0, 0)
         first_w = [expert_weights(e) for e in range(LEAD)]
-        for s in range(N_GATHER):
-            quantise_x(0, s)
+        quantise_x(0, 0)
         for e in range(LEAD):
             quantise_w(e, first_w[e])
         for s in range(N_GATHER):
@@ -158,7 +176,7 @@ def tile_routed_moe_kernel(tc, xT, w, b, gate, offs, out):
                 nc.vector.tensor_tensor(
                     windows[h][:].indirect(offsets[:, e * C // 16 : (e + 1) * C // 16]),
                     ys[h][:],
-                    gates[h][:, e * C : (e + 1) * C],
+                    gates[e // GATE_EXPERTS][:, h, (e % GATE_EXPERTS) * C : (e % GATE_EXPERTS + 1) * C],
                     MULT,
                 )
         for h in range(HALVES):

@@ -64,14 +64,11 @@ def tile_routed_moe_kernel(tc, xT, w, b, gate, offs, out):
         for e in range(E):
             if e == GATES_AFTER:
                 load_gate(0)
-            if e < E - 1:
-                nc.sync.dma_start(w_raw[e][:], w[e].rearrange("(g p j) n -> p g j n", p=P, j=PACK))
-            else:
-                for g in range(PASSES):
-                    nc.sync.dma_start(
-                        w_raw[e][:, g, :, :],
-                        w[e, g * K_PASS : (g + 1) * K_PASS, :].rearrange("(p j) n -> p j n", j=PACK),
-                    )
+            for g in range(PASSES):
+                nc.sync.dma_start(
+                    w_raw[e][:, g, :, :],
+                    w[e, g * K_PASS : (g + 1) * K_PASS, :].rearrange("(p j) n -> p j n", j=PACK),
+                )
         load_gate(1)
 
         warm = keep.tile([P, 1], F32, name="warm")
@@ -139,7 +136,12 @@ def tile_routed_moe_kernel(tc, xT, w, b, gate, offs, out):
 
         for t in range(PACK):
             nc.vector.tensor_copy(pairs[0][0][:, t // 2, :, t % 2], planes[0][t][:].indirect(list_slice(0, 0)))
-            nc.gpsimd.tensor_scalar(out=x16[:, t, :], in0=planes[1][t][:], scalar1=1.0, scalar2=0.0, op0=MULT, op1=ADD)
+            shared_cols = T // 2 if t == 0 else 0
+            if shared_cols:
+                nc.scalar.copy(out=x16[:, t, :shared_cols], in_=planes[1][t][:, :shared_cols])
+            nc.gpsimd.tensor_scalar(
+                out=x16[:, t, shared_cols:], in0=planes[1][t][:, shared_cols:], scalar1=1.0, scalar2=0.0, op0=MULT, op1=ADD
+            )
             for s in range(N_GATHER):
                 nc.scalar.activation(out=pairs[1][s][:, t // 2, :, t % 2], in_=x16[:, t, :].indirect(list_slice(1, s)), func=COPY)
         for s in range(N_GATHER):

@@ -31,6 +31,7 @@ GATE_PARTS = 2
 GATE_EXPERTS = E // GATE_PARTS
 W_BYTES = PASSES * PACK * N * 4
 Y_BYTES = C * 4
+FRONT = W_BYTES // PASSES
 
 
 def tile_routed_moe_kernel(tc, xT, w, b, gate, offs, out):
@@ -60,13 +61,18 @@ def tile_routed_moe_kernel(tc, xT, w, b, gate, offs, out):
         def load_gate(part):
             nc.sync.dma_start(gates[part][:], gate_view[:, :, part * GATE_EXPERTS * C : (part + 1) * GATE_EXPERTS * C])
 
-        w_raw = [shared.tile([P, PASSES, PACK, N], F32, name="wraw%d" % e, offset=e * W_BYTES) for e in range(E)]
+        w_first = [shared.tile([P, PACK, N], F32, name="wfirst%d" % g, offset=FRONT + g * W_BYTES // PASSES) for g in range(PASSES)]
+        w_raw = [None] + [shared.tile([P, PASSES, PACK, N], F32, name="wraw%d" % e, offset=FRONT + e * W_BYTES) for e in range(1, E)]
+
+        def raw_block(e, g):
+            return w_raw[e][:, g, :, :] if e else w_first[g][:]
+
         for e in range(E):
             if e == GATES_AFTER:
                 load_gate(0)
             for g in range(PASSES):
                 nc.sync.dma_start(
-                    w_raw[e][:, g, :, :],
+                    raw_block(e, g),
                     w[e, g * K_PASS : (g + 1) * K_PASS, :].rearrange("(p j) n -> p j n", j=PACK),
                 )
         load_gate(1)
@@ -83,8 +89,8 @@ def tile_routed_moe_kernel(tc, xT, w, b, gate, offs, out):
         windows = [keep.tile([P, T], F32, name="window%d" % h) for h in range(HALVES)]
         units = [[(0, E * C)], [(s * GATHER, GATHER) for s in range(N_GATHER)]]
         x_bf = [
-            [keep.tile([P, n, PACK], BF16, name="x_bf%d%d" % (g, first), align_bytes=64) for first, n in units[g]]
-            for g in range(PASSES)
+            [shared.tile([P, E * C, PACK], BF16, name="x_bf00", align_bytes=64, offset=0)],
+            [keep.tile([P, n, PACK], BF16, name="x_bf1%d" % first, align_bytes=64) for first, n in units[1]],
         ]
         x16 = keep.tile([P, PACK, T], BF16, name="x16")
         pairs = [
@@ -113,7 +119,7 @@ def tile_routed_moe_kernel(tc, xT, w, b, gate, offs, out):
 
         def expert_weights(e):
             w_bf = ring.tile([P, PASSES, N, PACK], BF16, name="w_bf", align_bytes=64)
-            if all((e, g) in VECTOR_BLOCKS for g in range(PASSES)):
+            if e and all((e, g) in VECTOR_BLOCKS for g in range(PASSES)):
                 nc.vector.tensor_copy(
                     out=w_bf[:].rearrange("p g (c i) t -> p g c t i", i=4),
                     in_=w_raw[e][:].rearrange("p g t (c i) -> p g c t i", i=4),
@@ -123,9 +129,15 @@ def tile_routed_moe_kernel(tc, xT, w, b, gate, offs, out):
                 copy = nc.vector.tensor_copy if (e, g) in VECTOR_BLOCKS else nc.scalar.copy
                 copy(
                     out=w_bf[:, g, :, :].rearrange("p (c i) t -> p c t i", i=4),
-                    in_=w_raw[e][:, g, :, :].rearrange("p t (c i) -> p c t i", i=4),
+                    in_=raw_block(e, g).rearrange("p t (c i) -> p c t i", i=4),
                 )
             return w_bf
+
+        def first_block(g, w_bf):
+            nc.vector.tensor_copy(
+                out=w_bf[:, g, :, :].rearrange("p (c i) t -> p c t i", i=4),
+                in_=raw_block(0, g).rearrange("p t (c i) -> p c t i", i=4),
+            )
 
         def quantise_w(e, w_bf):
             nc.vector.quantize_mx(
@@ -146,13 +158,16 @@ def tile_routed_moe_kernel(tc, xT, w, b, gate, offs, out):
                 nc.scalar.activation(out=pairs[1][s][:, t // 2, :, t % 2], in_=x16[:, t, :].indirect(list_slice(1, s)), func=COPY)
         for s in range(N_GATHER):
             weave(nc.scalar.copy, 1, s)
+        w_bf0 = ring.tile([P, PASSES, N, PACK], BF16, name="w_bf", align_bytes=64)
+        first_block(0, w_bf0)
         weave(nc.vector.tensor_copy, 0, 0)
-        first_w = [expert_weights(e) for e in range(LEAD)]
+        first_block(1, w_bf0)
         quantise_x(0, 0)
-        for e in range(LEAD):
-            quantise_w(e, first_w[e])
-        for s in range(N_GATHER):
-            quantise_x(1, s)
+        quantise_w(0, w_bf0)
+        quantise_x(1, 0)
+        w_bf1 = expert_weights(1)
+        quantise_x(1, 1)
+        quantise_w(1, w_bf1)
 
         for e in range(E):
             if e + LEAD < E:
@@ -170,7 +185,7 @@ def tile_routed_moe_kernel(tc, xT, w, b, gate, offs, out):
                         start=(g == 0),
                         stop=(g == PASSES - 1),
                     )
-                place = min(e + LEAD + 1, E + 1) * W_BYTES - (HALVES - h) * Y_BYTES if e + LEAD < E else E * W_BYTES + ((e + LEAD - E) * HALVES + h) * Y_BYTES
+                place = FRONT + (min(e + LEAD + 1, E + 1) * W_BYTES - (HALVES - h) * Y_BYTES if e + LEAD < E else E * W_BYTES + ((e + LEAD - E) * HALVES + h) * Y_BYTES)
                 y = shared.tile([P, C], F32, name="y%d%d" % (e, h), offset=place)
                 nc.scalar.activation(out=y[:], in_=acc[:], func=RELU, bias=bias[:, h, e : e + 1])
                 ys.append(y)

@@ -31,6 +31,7 @@ GATE_PARTS = 2
 GATE_EXPERTS = E // GATE_PARTS
 W_BYTES = PASSES * PACK * N * 4
 Y_BYTES = C * 4
+SPARE = W_BYTES // PASSES + E * W_BYTES
 FRONT = W_BYTES // PASSES
 
 
@@ -77,6 +78,9 @@ def tile_routed_moe_kernel(tc, xT, w, b, gate, offs, out):
                 )
         load_gate(1)
 
+        late_bias = shared.tile([P, HALVES], F32, name="late_bias", offset=SPARE + HALVES * Y_BYTES)
+        nc.gpsimd.tensor_copy(out=late_bias[:], in_=bias[:, :, E - 3])
+
         warm = keep.tile([P, 1], F32, name="warm")
         nc.vector.memset(warm[:], 0.0)
         warm_out = keep.tile([P, 1], F32, name="warm_out")
@@ -118,7 +122,10 @@ def tile_routed_moe_kernel(tc, xT, w, b, gate, offs, out):
             )
 
         def expert_weights(e):
-            w_bf = ring.tile([P, PASSES, N, PACK], BF16, name="w_bf", align_bytes=64)
+            if e == E - 1:
+                w_bf = shared.tile([P, PASSES, N, PACK], BF16, name="w_bf_last", align_bytes=64, offset=SPARE + HALVES * Y_BYTES)
+            else:
+                w_bf = ring.tile([P, PASSES, N, PACK], BF16, name="w_bf", align_bytes=64)
             if e and all((e, g) in VECTOR_BLOCKS for g in range(PASSES)):
                 nc.vector.tensor_copy(
                     out=w_bf[:].rearrange("p g (c i) t -> p g c t i", i=4),
@@ -170,8 +177,10 @@ def tile_routed_moe_kernel(tc, xT, w, b, gate, offs, out):
         quantise_w(1, w_bf1)
 
         for e in range(E):
-            if e + LEAD < E:
+            if e + LEAD < E - 1:
                 quantise_w(e + LEAD, expert_weights(e + LEAD))
+            if e == E - 2:
+                quantise_w(E - 1, expert_weights(E - 1))
             ys = []
             for h in range(HALVES):
                 acc = psum.tile([P, C], F32, name="acc")
@@ -185,9 +194,18 @@ def tile_routed_moe_kernel(tc, xT, w, b, gate, offs, out):
                         start=(g == 0),
                         stop=(g == PASSES - 1),
                     )
-                place = FRONT + (min(e + LEAD + 1, E + 1) * W_BYTES - (HALVES - h) * Y_BYTES if e + LEAD < E else E * W_BYTES + ((e + LEAD - E) * HALVES + h) * Y_BYTES)
+                if e < E - 3:
+                    place = FRONT + (e + LEAD + 1) * W_BYTES - (HALVES - h) * Y_BYTES
+                elif e == E - 3:
+                    place = FRONT + (e + 2) * W_BYTES - (2 * HALVES - h) * Y_BYTES
+                elif e == E - 2:
+                    place = FRONT + (e + 2) * W_BYTES - (HALVES - h) * Y_BYTES
+                else:
+                    place = SPARE + h * Y_BYTES
                 y = shared.tile([P, C], F32, name="y%d%d" % (e, h), offset=place)
-                nc.scalar.activation(out=y[:], in_=acc[:], func=RELU, bias=bias[:, h, e : e + 1])
+                nc.scalar.activation(
+                    out=y[:], in_=acc[:], func=RELU, bias=late_bias[:, h : h + 1] if e == E - 3 else bias[:, h, e : e + 1]
+                )
                 ys.append(y)
             for h in range(HALVES):
                 nc.vector.tensor_tensor(

@@ -26,8 +26,8 @@ N_GATHER = E * C // GATHER
 LEAD = 2
 VECTOR_BLOCKS = ((0, 0), (0, 1), (1, 0), (1, 1), (4, 0))
 WINDOW = T * 11 // 8
-GATES_AFTER = 3
-GATE_PARTS = 2
+GATE_PARTS = 4
+GATE_BEFORE = {3: 0, 5: 1, 7: 2}
 GATE_EXPERTS = E // GATE_PARTS
 W_BYTES = PASSES * PACK * N * 4
 Y_BYTES = C * 4
@@ -69,14 +69,14 @@ def tile_routed_moe_kernel(tc, xT, w, b, gate, offs, out):
             return w_raw[e][:, g, :, :] if e else w_first[g][:]
 
         for e in range(E):
-            if e == GATES_AFTER:
-                load_gate(0)
+            if e in GATE_BEFORE:
+                load_gate(GATE_BEFORE[e])
             for g in range(PASSES):
                 nc.sync.dma_start(
                     raw_block(e, g),
                     w[e, g * K_PASS : (g + 1) * K_PASS, :].rearrange("(p j) n -> p j n", j=PACK),
                 )
-        load_gate(1)
+        load_gate(GATE_PARTS - 1)
 
         late_bias = shared.tile([P, HALVES], F32, name="late_bias", offset=SPARE + HALVES * Y_BYTES)
         nc.gpsimd.tensor_copy(out=late_bias[:], in_=bias[:, :, E - 3])

@@ -122,10 +122,7 @@ def tile_routed_moe_kernel(tc, xT, w, b, gate, offs, out):
             )
 
         def expert_weights(e):
-            if e == E - 1:
-                w_bf = shared.tile([P, PASSES, N, PACK], BF16, name="w_bf_last", align_bytes=64, offset=SPARE + HALVES * Y_BYTES)
-            else:
-                w_bf = ring.tile([P, PASSES, N, PACK], BF16, name="w_bf", align_bytes=64)
+            w_bf = ring.tile([P, PASSES, N, PACK], BF16, name="w_bf", align_bytes=64)
             if e and all((e, g) in VECTOR_BLOCKS for g in range(PASSES)):
                 nc.vector.tensor_copy(
                     out=w_bf[:].rearrange("p g (c i) t -> p g c t i", i=4),
@@ -145,6 +142,20 @@ def tile_routed_moe_kernel(tc, xT, w, b, gate, offs, out):
                 out=w_bf[:, g, :, :].rearrange("p (c i) t -> p c t i", i=4),
                 in_=raw_block(0, g).rearrange("p t (c i) -> p c t i", i=4),
             )
+
+        def last_weights():
+            e = E - 1
+            w_bf = shared.tile([P, PASSES, N, PACK], BF16, name="w_bf_last", align_bytes=64, offset=SPARE + HALVES * Y_BYTES)
+            for g in range(PASSES):
+                nc.scalar.copy(
+                    out=w_bf[:, g, :, :].rearrange("p (c i) t -> p c t i", i=4),
+                    in_=raw_block(e, g).rearrange("p t (c i) -> p c t i", i=4),
+                )
+                nc.vector.quantize_mx(
+                    out=w_codes[e][:, g, :].bitcast(FP8X4),
+                    scales=w_scales[e][:, g, :],
+                    in_=w_bf[:, g, :, :].rearrange("p c t -> p (c t)"),
+                )
 
         def quantise_w(e, w_bf):
             nc.vector.quantize_mx(
@@ -176,30 +187,43 @@ def tile_routed_moe_kernel(tc, xT, w, b, gate, offs, out):
         quantise_x(1, 1)
         quantise_w(1, w_bf1)
 
+        def multiply(acc, e, h, g):
+            nc.tensor.matmul_mx(
+                out=acc[:],
+                lhsT=w_codes[e][:, g, h * P : (h + 1) * P].bitcast(FP8X4),
+                lhsT_scale=w_scales[e][:, g, h * P : (h + 1) * P],
+                rhs=x_codes[:, g, e * C : (e + 1) * C].bitcast(FP8X4),
+                rhs_scale=x_scales[:, g, e * C : (e + 1) * C],
+                start=(g == 0),
+                stop=(g == PASSES - 1),
+            )
+
         for e in range(E):
             if e + LEAD < E - 1:
                 quantise_w(e + LEAD, expert_weights(e + LEAD))
             if e == E - 2:
-                quantise_w(E - 1, expert_weights(E - 1))
+                last_weights()
             ys = []
+            early = []
+            if e == E - 1:
+                for h in range(HALVES):
+                    acc = psum.tile([P, C], F32, name="acc")
+                    multiply(acc, e, h, 0)
+                    early.append(acc)
             for h in range(HALVES):
-                acc = psum.tile([P, C], F32, name="acc")
-                for g in range(PASSES):
-                    nc.tensor.matmul_mx(
-                        out=acc[:],
-                        lhsT=w_codes[e][:, g, h * P : (h + 1) * P].bitcast(FP8X4),
-                        lhsT_scale=w_scales[e][:, g, h * P : (h + 1) * P],
-                        rhs=x_codes[:, g, e * C : (e + 1) * C].bitcast(FP8X4),
-                        rhs_scale=x_scales[:, g, e * C : (e + 1) * C],
-                        start=(g == 0),
-                        stop=(g == PASSES - 1),
-                    )
+                if early:
+                    acc = early[h]
+                    multiply(acc, e, h, 1)
+                else:
+                    acc = psum.tile([P, C], F32, name="acc")
+                    for g in range(PASSES):
+                        multiply(acc, e, h, g)
                 if e < E - 3:
                     place = FRONT + (e + LEAD + 1) * W_BYTES - (HALVES - h) * Y_BYTES
                 elif e == E - 3:
                     place = FRONT + (e + 2) * W_BYTES - (2 * HALVES - h) * Y_BYTES
                 elif e == E - 2:
-                    place = FRONT + (e + 2) * W_BYTES - (HALVES - h) * Y_BYTES
+                    place = FRONT + (e + 2) * W_BYTES - Y_BYTES if h else SPARE + HALVES * Y_BYTES + W_BYTES // 2
                 else:
                     place = SPARE + h * Y_BYTES
                 y = shared.tile([P, C], F32, name="y%d%d" % (e, h), offset=place)

@@ -24,6 +24,7 @@ HALVES = N // P
 GATHER = 512
 N_GATHER = E * C // GATHER
 LEAD = 2
+SWITCH = 4
 VECTOR_BLOCKS = ((0, 0), (0, 1), (1, 0), (1, 1), (4, 0))
 WINDOW = T * 11 // 8
 GATE_PARTS = 4
@@ -78,8 +79,13 @@ def tile_routed_moe_kernel(tc, xT, w, b, gate, offs, out):
                 )
         load_gate(GATE_PARTS - 1)
 
-        late_bias = shared.tile([P, HALVES], F32, name="late_bias", offset=SPARE + HALVES * Y_BYTES)
-        nc.gpsimd.tensor_copy(out=late_bias[:], in_=bias[:, :, E - 3])
+        def late_place(e):
+            return SPARE + (HALVES + 1) * Y_BYTES + (E - 3 - e) * W_BYTES // 2
+
+        late_bias = {}
+        for e in range(SWITCH, E - 2):
+            late_bias[e] = shared.tile([P, HALVES], F32, name="late_bias%d" % e, offset=late_place(e))
+            nc.gpsimd.tensor_copy(out=late_bias[e][:], in_=bias[:, :, e])
 
         warm = keep.tile([P, 1], F32, name="warm")
         nc.vector.memset(warm[:], 0.0)
@@ -122,7 +128,10 @@ def tile_routed_moe_kernel(tc, xT, w, b, gate, offs, out):
             )
 
         def expert_weights(e):
-            w_bf = ring.tile([P, PASSES, N, PACK], BF16, name="w_bf", align_bytes=64)
+            if e - 2 in late_bias:
+                w_bf = shared.tile([P, PASSES, N, PACK], BF16, name="w_bf%d" % e, align_bytes=64, offset=late_place(e - 2))
+            else:
+                w_bf = ring.tile([P, PASSES, N, PACK], BF16, name="w_bf", align_bytes=64)
             if e and all((e, g) in VECTOR_BLOCKS for g in range(PASSES)):
                 nc.vector.tensor_copy(
                     out=w_bf[:].rearrange("p g (c i) t -> p g c t i", i=4),
@@ -145,7 +154,7 @@ def tile_routed_moe_kernel(tc, xT, w, b, gate, offs, out):
 
         def last_weights():
             e = E - 1
-            w_bf = shared.tile([P, PASSES, N, PACK], BF16, name="w_bf_last", align_bytes=64, offset=SPARE + HALVES * Y_BYTES)
+            w_bf = shared.tile([P, PASSES, N, PACK], BF16, name="w_bf_last", align_bytes=64, offset=late_place(e - 2))
             for g in range(PASSES):
                 nc.scalar.copy(
                     out=w_bf[:, g, :, :].rearrange("p (c i) t -> p c t i", i=4),
@@ -199,9 +208,11 @@ def tile_routed_moe_kernel(tc, xT, w, b, gate, offs, out):
             )
 
         for e in range(E):
-            if e + LEAD < E - 1:
+            if e < SWITCH:
                 quantise_w(e + LEAD, expert_weights(e + LEAD))
-            if e == E - 2:
+            elif SWITCH < e < E - 2:
+                quantise_w(e + 1, expert_weights(e + 1))
+            elif e == E - 2:
                 last_weights()
             ys = []
             early = []
@@ -218,17 +229,19 @@ def tile_routed_moe_kernel(tc, xT, w, b, gate, offs, out):
                     acc = psum.tile([P, C], F32, name="acc")
                     for g in range(PASSES):
                         multiply(acc, e, h, g)
-                if e < E - 3:
+                if e < SWITCH:
                     place = FRONT + (e + LEAD + 1) * W_BYTES - (HALVES - h) * Y_BYTES
-                elif e == E - 3:
+                elif e == SWITCH:
                     place = FRONT + (e + 2) * W_BYTES - (2 * HALVES - h) * Y_BYTES
+                elif e < E - 2:
+                    place = FRONT + (e + 2) * W_BYTES - (HALVES - h) * Y_BYTES
                 elif e == E - 2:
-                    place = FRONT + (e + 2) * W_BYTES - Y_BYTES if h else SPARE + HALVES * Y_BYTES + W_BYTES // 2
+                    place = FRONT + (e + 2) * W_BYTES - Y_BYTES if h else SPARE + HALVES * Y_BYTES
                 else:
                     place = SPARE + h * Y_BYTES
                 y = shared.tile([P, C], F32, name="y%d%d" % (e, h), offset=place)
                 nc.scalar.activation(
-                    out=y[:], in_=acc[:], func=RELU, bias=late_bias[:, h : h + 1] if e == E - 3 else bias[:, h, e : e + 1]
+                    out=y[:], in_=acc[:], func=RELU, bias=late_bias[e][:, h : h + 1] if e in late_bias else bias[:, h, e : e + 1]
                 )
                 ys.append(y)
             for h in range(HALVES):

from contextlib import ExitStack

import concourse.mybir as mybir

K, T, E, C, N = 1024, 1024, 8, 128, 256
FLOPS = 2 * E * C * K * N

F32 = mybir.dt.float32
BF16 = mybir.dt.bfloat16
U32 = mybir.dt.uint32
U16 = mybir.dt.uint16
U8 = mybir.dt.uint8
FP8X4 = mybir.dt.float8_e4m3fn_x4
MULT = mybir.AluOpType.mult
ADD = mybir.AluOpType.add
RELU = mybir.ActivationFunctionType.Relu
COPY = mybir.ActivationFunctionType.Copy

P = 128
PACK = 4
K_PASS = P * PACK
PASSES = K // K_PASS
HALVES = N // P
GATHER = 512
N_GATHER = E * C // GATHER
LEAD = 2
SWITCH = 4
VECTOR_BLOCKS = ((0, 0), (0, 1), (1, 0), (1, 1), (4, 0))
WINDOW = T * 11 // 8
GATE_PARTS = 4
GATE_BEFORE = {3: 0, 5: 1, 7: 2}
GATE_EXPERTS = E // GATE_PARTS
W_BYTES = PASSES * PACK * N * 4
Y_BYTES = C * 4
SPARE = W_BYTES // PASSES + E * W_BYTES
FRONT = W_BYTES // PASSES


def tile_routed_moe_kernel(tc, xT, w, b, gate, offs, out):
    nc = tc.nc
    with ExitStack() as ctx:
        keep = ctx.enter_context(tc.tile_pool(name="keep", bufs=1))
        shared = ctx.enter_context(tc.tile_pool(name="shared", bufs=1))
        ring = ctx.enter_context(tc.tile_pool(name="ring", bufs=6))
        psum = ctx.enter_context(tc.psum_pool(name="psum", bufs=8))

        offsets = keep.tile([P, E * C // 16], U16, name="offsets")
        nc.sync.dma_start(offsets[:], offs)

        x_view = xT.rearrange("(g p t) n -> g p t n", p=P, t=PACK)
        planes = [[keep.tile([P, T if g else WINDOW], F32, name="plane%d%d" % (g, t)) for t in range(PACK)] for g in range(PASSES)]
        for t in range(PACK):
            nc.gpsimd.memset(planes[0][t][:, T:], 0.0)
        for t in range(PACK):
            for g in range(PASSES):
                nc.sync.dma_start(planes[g][t][:, :T], x_view[g, :, t, :])

        bias = keep.tile([P, HALVES, E], F32, name="bias")
        nc.sync.dma_start(bias[:], b.rearrange("(h p) e -> p h e", p=P))
        gates = [keep.tile([P, HALVES, GATE_EXPERTS * C], F32, name="gates%d" % part) for part in range(GATE_PARTS)]
        gate_view = gate.rearrange("(h p) s -> p h s", p=P)

        def load_gate(part):
            nc.sync.dma_start(gates[part][:], gate_view[:, :, part * GATE_EXPERTS * C : (part + 1) * GATE_EXPERTS * C])

        w_first = [shared.tile([P, PACK, N], F32, name="wfirst%d" % g, offset=FRONT + g * W_BYTES // PASSES) for g in range(PASSES)]
        w_raw = [None] + [shared.tile([P, PASSES, PACK, N], F32, name="wraw%d" % e, offset=FRONT + e * W_BYTES) for e in range(1, E)]

        def raw_block(e, g):
            return w_raw[e][:, g, :, :] if e else w_first[g][:]

        for e in range(E):
            if e in GATE_BEFORE:
                load_gate(GATE_BEFORE[e])
            for g in range(PASSES):
                nc.sync.dma_start(
                    raw_block(e, g),
                    w[e, g * K_PASS : (g + 1) * K_PASS, :].rearrange("(p j) n -> p j n", j=PACK),
                )
        load_gate(GATE_PARTS - 1)

        def late_place(e):
            return SPARE + (HALVES + 1) * Y_BYTES + (E - 3 - e) * W_BYTES // 2

        late_bias = {}
        for e in range(SWITCH, E - 2):
            late_bias[e] = shared.tile([P, HALVES], F32, name="late_bias%d" % e, offset=late_place(e))
            nc.gpsimd.tensor_copy(out=late_bias[e][:], in_=bias[:, :, e])

        warm = keep.tile([P, 1], F32, name="warm")
        nc.vector.memset(warm[:], 0.0)
        warm_out = keep.tile([P, 1], F32, name="warm_out")
        nc.scalar.activation(out=warm_out[:], in_=warm[:], func=RELU)

        x_codes = keep.tile([P, PASSES, E * C], U32, name="x_codes", align_bytes=64)
        x_scales = keep.tile([P, PASSES, E * C], U8, name="x_scales", align_bytes=64)
        w_codes = [keep.tile([P, PASSES, N], U32, name="w_codes%d" % e, align_bytes=64) for e in range(E)]
        w_scales = [keep.tile([P, PASSES, N], U8, name="w_scales%d" % e, align_bytes=64) for e in range(E)]
        windows = [keep.tile([P, T], F32, name="window%d" % h) for h in range(HALVES)]
        units = [[(0, E * C)], [(s * GATHER, GATHER) for s in range(N_GATHER)]]
        x_bf = [
            [shared.tile([P, E * C, PACK], BF16, name="x_bf00", align_bytes=64, offset=0)],
            [keep.tile([P, n, PACK], BF16, name="x_bf1%d" % first, align_bytes=64) for first, n in units[1]],
        ]
        x16 = keep.tile([P, PACK, T], BF16, name="x16")
        pairs = [
            [keep.tile([P, PACK // 2, n, 2], BF16, name="pairs%d%d" % (g, first), align_bytes=64) for first, n in units[g]]
            for g in range(PASSES)
        ]

        def weave(copy, g, s):
            copy(
                out=x_bf[g][s][:].rearrange("p c t -> p (c t)").bitcast(F32).rearrange("p (c u) -> p c u", u=2),
                in_=pairs[g][s][:].rearrange("p u c i -> p (u c i)").bitcast(F32).rearrange("p (u c) -> p c u", u=2),
            )

        def list_slice(g, s):
            first, n = units[g][s]
            return offsets[:, first // 16 : (first + n) // 16]

        def quantise_x(g, s):
            first, n = units[g][s]
            cols = slice(first, first + n)
            nc.vector.quantize_mx(
                out=x_codes[:, g, cols].bitcast(FP8X4),
                scales=x_scales[:, g, cols],
                in_=x_bf[g][s][:].rearrange("p c t -> p (c t)"),
            )

        def expert_weights(e):
            if e - 2 in late_bias:
                w_bf = shared.tile([P, PASSES, N, PACK], BF16, name="w_bf%d" % e, align_bytes=64, offset=late_place(e - 2))
            else:
                w_bf = ring.tile([P, PASSES, N, PACK], BF16, name="w_bf", align_bytes=64)
            if e and all((e, g) in VECTOR_BLOCKS for g in range(PASSES)):
                nc.vector.tensor_copy(
                    out=w_bf[:].rearrange("p g (c i) t -> p g c t i", i=4),
                    in_=w_raw[e][:].rearrange("p g t (c i) -> p g c t i", i=4),
                )
                return w_bf
            for g in range(PASSES):
                copy = nc.vector.tensor_copy if (e, g) in VECTOR_BLOCKS else nc.scalar.copy
                copy(
                    out=w_bf[:, g, :, :].rearrange("p (c i) t -> p c t i", i=4),
                    in_=raw_block(e, g).rearrange("p t (c i) -> p c t i", i=4),
                )
            return w_bf

        def first_block(g, w_bf):
            nc.vector.tensor_copy(
                out=w_bf[:, g, :, :].rearrange("p (c i) t -> p c t i", i=4),
                in_=raw_block(0, g).rearrange("p t (c i) -> p c t i", i=4),
            )

        def last_weights():
            e = E - 1
            w_bf = shared.tile([P, PASSES, N, PACK], BF16, name="w_bf_last", align_bytes=64, offset=late_place(e - 2))
            for g in range(PASSES):
                nc.scalar.copy(
                    out=w_bf[:, g, :, :].rearrange("p (c i) t -> p c t i", i=4),
                    in_=raw_block(e, g).rearrange("p t (c i) -> p c t i", i=4),
                )
                nc.vector.quantize_mx(
                    out=w_codes[e][:, g, :].bitcast(FP8X4),
                    scales=w_scales[e][:, g, :],
                    in_=w_bf[:, g, :, :].rearrange("p c t -> p (c t)"),
                )

        def quantise_w(e, w_bf):
            nc.vector.quantize_mx(
                out=w_codes[e][:].rearrange("p g n -> p (g n)").bitcast(FP8X4),
                scales=w_scales[e][:].rearrange("p g n -> p (g n)"),
                in_=w_bf[:].rearrange("p g c t -> p (g c t)"),
            )

        for t in range(PACK):
            nc.vector.tensor_copy(pairs[0][0][:, t // 2, :, t % 2], planes[0][t][:].indirect(list_slice(0, 0)))
            shared_cols = T // 2 if t == 0 else 0
            if shared_cols:
                nc.scalar.copy(out=x16[:, t, :shared_cols], in_=planes[1][t][:, :shared_cols])
            nc.gpsimd.tensor_scalar(
                out=x16[:, t, shared_cols:], in0=planes[1][t][:, shared_cols:], scalar1=1.0, scalar2=0.0, op0=MULT, op1=ADD
            )
            for s in range(N_GATHER):
                nc.scalar.activation(out=pairs[1][s][:, t // 2, :, t % 2], in_=x16[:, t, :].indirect(list_slice(1, s)), func=COPY)
        for s in range(N_GATHER):
            weave(nc.scalar.copy, 1, s)
        w_bf0 = ring.tile([P, PASSES, N, PACK], BF16, name="w_bf", align_bytes=64)
        first_block(0, w_bf0)
        weave(nc.vector.tensor_copy, 0, 0)
        first_block(1, w_bf0)
        quantise_x(0, 0)
        quantise_w(0, w_bf0)
        quantise_x(1, 0)
        w_bf1 = expert_weights(1)
        quantise_x(1, 1)
        quantise_w(1, w_bf1)

        def multiply(acc, e, h, g):
            nc.tensor.matmul_mx(
                out=acc[:],
                lhsT=w_codes[e][:, g, h * P : (h + 1) * P].bitcast(FP8X4),
                lhsT_scale=w_scales[e][:, g, h * P : (h + 1) * P],
                rhs=x_codes[:, g, e * C : (e + 1) * C].bitcast(FP8X4),
                rhs_scale=x_scales[:, g, e * C : (e + 1) * C],
                start=(g == 0),
                stop=(g == PASSES - 1),
            )

        for e in range(E):
            if e < SWITCH:
                quantise_w(e + LEAD, expert_weights(e + LEAD))
            elif SWITCH < e < E - 2:
                quantise_w(e + 1, expert_weights(e + 1))
            elif e == E - 2:
                last_weights()
            ys = []
            early = []
            if e == E - 1:
                for h in range(HALVES):
                    acc = psum.tile([P, C], F32, name="acc")
                    multiply(acc, e, h, 0)
                    early.append(acc)
            for h in range(HALVES):
                if early:
                    acc = early[h]
                    multiply(acc, e, h, 1)
                else:
                    acc = psum.tile([P, C], F32, name="acc")
                    for g in range(PASSES):
                        multiply(acc, e, h, g)
                if e < SWITCH:
                    place = FRONT + (e + LEAD + 1) * W_BYTES - (HALVES - h) * Y_BYTES
                elif e == SWITCH:
                    place = FRONT + (e + 2) * W_BYTES - (2 * HALVES - h) * Y_BYTES
                elif e < E - 2:
                    place = FRONT + (e + 2) * W_BYTES - (HALVES - h) * Y_BYTES
                elif e == E - 2:
                    place = FRONT + (e + 2) * W_BYTES - Y_BYTES if h else SPARE + HALVES * Y_BYTES
                else:
                    place = SPARE + h * Y_BYTES
                y = shared.tile([P, C], F32, name="y%d%d" % (e, h), offset=place)
                nc.scalar.activation(
                    out=y[:], in_=acc[:], func=RELU, bias=late_bias[e][:, h : h + 1] if e in late_bias else bias[:, h, e : e + 1]
                )
                ys.append(y)
            for h in range(HALVES):
                nc.vector.tensor_tensor(
                    windows[h][:].indirect(offsets[:, e * C // 16 : (e + 1) * C // 16]),
                    ys[h][:],
                    gates[e // GATE_EXPERTS][:, h, (e % GATE_EXPERTS) * C : (e % GATE_EXPERTS + 1) * C],
                    MULT,
                )
        for h in range(HALVES):
            nc.sync.dma_start(out[h * P : (h + 1) * P, :], windows[h][:])
